import numpy as np
import ml_dtypes


def mxq(x, axis, fmt="e4m3"):
    dtype, down = {"e4m3": (ml_dtypes.float8_e4m3fn, 7), "e5m2": (ml_dtypes.float8_e5m2, 14)}[fmt]
    v = np.moveaxis(np.asarray(x, np.float32).astype(ml_dtypes.bfloat16).astype(np.float64), axis, -1)
    blocks = v.reshape(v.shape[:-1] + (-1, 32))
    amax = np.abs(blocks).max(-1, keepdims=True)
    byte = np.maximum(np.where(amax > 0, np.frexp(amax)[1] - 1 + 127, 0) - down, 1)
    scale = np.exp2(byte - 127.0)
    codes = (blocks / scale).astype(np.float32).astype(dtype).astype(np.float64)
    return np.moveaxis((codes * scale).reshape(v.shape), -1, axis)


WIDE = False


def mx_kscale(k):
    if not WIDE:
        return np.ones(k)
    levels = np.array([24, -24, 12, -12, 0])
    if k % 512:
        return np.exp2(np.random.permutation(np.resize(levels, k // 32))).repeat(32)
    a = np.empty((k // 512, 16))
    for p in range(k // 512):
        a[p, :8] = np.random.permutation(np.resize(levels, 8))
        for g in range(8):
            far = levels[np.abs(levels - a[p, g]) >= 10]
            a[p, g + 8] = far[np.random.randint(len(far))]
    return np.exp2(a.ravel()).repeat(32)


def f64(x):
    return np.asarray(x).astype(np.float64)


def striped8(idx):
    return np.concatenate([v.reshape(-1, 16).T for v in idx]).astype(np.uint16)


def unstriped8(offs):
    return np.stack([offs[16 * g:16 * g + 16].T.reshape(-1) for g in range(8)]).astype(np.int64)


E2M1 = np.array([0.0, 0.5, 1.0, 1.5, 2.0, 3.0, 4.0, 6.0, -0.0, -0.5, -1.0, -1.5, -2.0, -3.0, -4.0, -6.0])


def pack_weight(w, fmt):
    k, n = w.shape
    w = f64(np.asarray(w, np.float32).astype(ml_dtypes.bfloat16)).reshape(k // 32, 32, n)
    amax = np.abs(w).max(1)
    if fmt == "e4m3":
        byte = np.frexp(amax)[1] - 1 + 127 - 7
    else:
        mant, ex = np.frexp(amax / 6.0)
        byte = np.where(mant > 0.5, ex, ex - 1) + 127
    byte = np.clip(np.where(amax > 0, byte, 1), 1, 254)
    scaled = (w * np.exp2(127.0 - byte)[:, None, :]).reshape(k, n).astype(np.float32)
    by_word = np.ascontiguousarray(scaled.reshape(k // 512, 128, 4, n).transpose(0, 1, 3, 2))
    if fmt == "e4m3":
        words = by_word.astype(ml_dtypes.float8_e4m3fn).view(np.uint8)
    else:
        c = by_word.astype(ml_dtypes.float4_e2m1fn).view(np.uint8) & 0xF
        words = (c[..., 0::2] | (c[..., 1::2] << 4)).reshape(k // 512, 128, 2 * n)
    return np.ascontiguousarray(words), np.ascontiguousarray(byte.astype(np.uint8).reshape(k // 512, 16, n))


def unpack_weight(words, scales, fmt):
    g, _, n = scales.shape
    words = np.ascontiguousarray(words).reshape(g, 128, n, -1)
    if fmt == "e4m3":
        vals = words.view(ml_dtypes.float8_e4m3fn).astype(np.float64)
    else:
        nib = np.empty((g, 128, n, 4), np.uint8)
        nib[..., 0::2] = words & 0xF
        nib[..., 1::2] = words >> 4
        vals = E2M1[nib]
    vals = vals * np.repeat(np.exp2(scales.astype(np.float64) - 127.0), 8, axis=1)[..., None]
    return vals.transpose(0, 1, 3, 2).reshape(g * 512, n)


def planes(y):
    n, m = y.shape
    v = y.astype(np.float32).astype(ml_dtypes.bfloat16).astype(np.float64).reshape(n // 32, 32, m)
    top = np.abs(v).max(1)
    byte = np.clip(np.where(top > 0, np.frexp(top)[1] - 1 + 127 - 7, 1), 1, 254)
    codes = (v * np.exp2(127.0 - byte)[:, None, :]).reshape(n, m).astype(np.float32).astype(ml_dtypes.float8_e4m3fn).view(np.uint8)
    words = codes.reshape(n // 512, 128, 4, m).transpose(0, 1, 3, 2)
    return np.ascontiguousarray(words), np.ascontiguousarray(byte.astype(np.uint8).reshape(n // 512, 16, m))


def silu(f):
    return f / (1.0 + np.exp(-np.maximum(f, -700.0)))


K, R, N, T, J = 1024, 1024, 512, 2048, 1024


def setup_inputs():
    n = np.random.standard_normal
    s = mx_kscale(K)[:, None]
    u = mx_kscale(R)[:, None]
    p_wg = pack_weight(n((K, R)) / np.sqrt(K) / s, "e2m1")
    p_wu = pack_weight(n((K, R)) / np.sqrt(K) / s * u.T, "e4m3")
    p_wd = pack_weight(n((R, N)) / np.sqrt(R) / u, "e4m3")
    return {
        "xT": (n((K, T)) * s).astype(np.float32),
        "wgt": np.repeat(np.random.uniform(0.5, 2.0, (8, J)), 16, axis=0).astype(np.float32),
        "wg_words": p_wg[0],
        "wg_scales": p_wg[1],
        "wu_words": p_wu[0],
        "wu_scales": p_wu[1],
        "wd_words": p_wd[0],
        "wd_scales": p_wd[1],
        "g": (n((N, J))).astype(np.float32),
        "offs": striped8(np.stack([np.random.permutation(T)[:J] for _ in range(8)])),
    }


def reference(xT, wgt, wg_words, wg_scales, wu_words, wu_scales, wd_words, wd_scales, g, offs):
    idx = unstriped8(offs)
    rows = np.arange(K)
    xg = f64(wgt)[rows // 4 % 128] * f64(xT)[rows[:, None], idx[rows % 512 // 64]]
    xT_ = mxq(xg, 0, "e4m3")
    wg_ = unpack_weight(wg_words, wg_scales, "e2m1")
    wu_ = unpack_weight(wu_words, wu_scales, "e4m3")
    ga = wg_.T @ xT_
    ub = wu_.T @ xT_
    h = silu(ga) * ub
    h_ = mxq(h, 0, "e4m3")
    wd_ = unpack_weight(wd_words, wd_scales, "e4m3")
    y = wd_.T @ h_
    out_0 = y * f64(g)
    return (out_0,) + planes(out_0)

@@ -1,0 +1,230 @@
+from contextlib import ExitStack
+
+import concourse.mybir as mybir
+from concourse.masks import make_identity
+
+K, R, N, T, J = 1024, 1024, 512, 2048, 1024
+FLOPS = 2 * J * (2 * K * R + R * N)
+
+F32 = mybir.dt.float32
+BF16 = mybir.dt.bfloat16
+I32 = mybir.dt.int32
+U32 = mybir.dt.uint32
+U16 = mybir.dt.uint16
+U8 = mybir.dt.uint8
+FP8X4 = mybir.dt.float8_e4m3fn_x4
+FP4X4 = mybir.dt.float4_e2m1fn_x4
+MULT = mybir.AluOpType.mult
+SILU = mybir.ActivationFunctionType.Silu
+
+P = 128
+PACK = 4
+BANK = 512
+CH = 256
+NCH = J // CH
+LANES = 16
+
+
+def weave(nc, dst, src):
+    nc.scalar.copy(
+        out=dst.rearrange("p (c i t) -> p c t i", i=PACK, t=PACK),
+        in_=src.rearrange("p t (c i) -> p c t i", i=PACK),
+    )
+
+
+def tile_list_silu_mulP_kernel(
+    tc, xT, wgt, wg_words, wg_scales, wu_words, wu_scales, wd_words, wd_scales, g, offs, out_0, out_1, out_2
+):
+    nc = tc.nc
+    with ExitStack() as ctx:
+        keep = ctx.enter_context(tc.tile_pool(name="keep", bufs=1))
+        ring = ctx.enter_context(tc.tile_pool(name="ring", bufs=4))
+        psum = ctx.enter_context(tc.psum_pool(name="psum", bufs=2))
+
+        offsets = keep.tile([P, J // LANES], U16, name="offsets")
+        nc.sync.dma_start(offsets[:], offs)
+
+        wg_s = keep.tile([P, 2, R], U8, name="wg_s", align_bytes=64)
+        wu_s = keep.tile([P, R], U8, name="wu_s", align_bytes=64)
+        wd_s_raw = keep.tile([P, N], U8, name="wd_s_raw", align_bytes=64)
+        nc.vector.memset(wg_s[:].rearrange("p a r -> p (a r)").bitcast(I32), 0)
+        nc.vector.memset(wu_s[:].bitcast(I32), 0)
+        nc.vector.memset(wd_s_raw[:].bitcast(I32), 0)
+
+        warm = keep.tile([P, 1], F32, name="warm")
+        nc.vector.memset(warm[:], 0.0)
+        warm_out = keep.tile([P, 1], F32, name="warm_out")
+        nc.scalar.activation(warm_out[:], warm[:], SILU)
+
+        ident = keep.tile([P, P], F32, name="ident")
+        make_identity(nc, ident[:])
+
+        x_rows = xT.rearrange("(a p i) t -> a i p t", a=2, i=PACK)
+        planes = {}
+
+        def load_plane(a, i):
+            planes[a, i] = keep.tile([P, T], F32, name="x%d%d" % (a, i))
+            nc.sync.dma_start(planes[a, i][:], x_rows[a, i])
+
+        load_plane(0, 0)
+        wgt_sb = keep.tile([P, J], F32, name="wgt_sb")
+        nc.sync.dma_start(wgt_sb[:], wgt)
+        for i in range(1, PACK):
+            load_plane(0, i)
+        for q in range(4):
+            nc.sync.dma_start(
+                wg_s[32 * q : 32 * q + 4].bitcast(I32),
+                wg_scales[:, 4 * q : 4 * q + 4, :].rearrange("a q r -> q a r").bitcast(I32),
+            )
+            nc.sync.dma_start(wu_s[32 * q : 32 * q + 8].bitcast(I32), wu_scales[:, 4 * q : 4 * q + 4, :].bitcast(I32))
+        for i in range(PACK - 1):
+            load_plane(1, i)
+        wg_w, wu_w = [], []
+
+        def load_w(h):
+            wg_w.append(keep.tile([P, 2, 2 * BANK], U8, name="wg_w%d" % h, align_bytes=64))
+            nc.sync.dma_start(
+                wg_w[h][:].bitcast(I32),
+                wg_words.rearrange("a p b -> p a b")[:, :, 2 * BANK * h : 2 * BANK * (h + 1)].bitcast(I32),
+            )
+            wu_w.append(keep.tile([P, 2, BANK], I32, name="wu_w%d" % h, align_bytes=64))
+            nc.sync.dma_start(
+                wu_w[h][:],
+                wu_words.rearrange("a p r i -> p a (r i)")[:, :, 4 * BANK * h : 4 * BANK * (h + 1)].bitcast(I32),
+            )
+
+        load_w(0)
+        load_plane(1, PACK - 1)
+        load_w(1)
+        for q in range(4):
+            nc.sync.dma_start(wd_s_raw[32 * q : 32 * q + 8].bitcast(I32), wd_scales[:, 4 * q : 4 * q + 4, :].bitcast(I32))
+        wd_raw = keep.tile([P, 2, N], I32, name="wd_raw", align_bytes=64)
+        nc.sync.dma_start(wd_raw[:], wd_words.rearrange("a p n i -> p a (n i)").bitcast(I32))
+        g_rows = g.rearrange("(p t) j -> p t j", t=PACK)
+        g_c = []
+        for c in range(NCH):
+            g_c.append(keep.tile([P, PACK, CH], F32, name="g%d" % c))
+            nc.sync.dma_start(g_c[c][:], g_rows[:, :, c * CH : (c + 1) * CH])
+
+        x_w, x_s = {}, {}
+
+        def quantise_x(a, c, picked):
+            woven = keep.tile([P, PACK * CH], BF16, name="xi%d%d" % (a, c), align_bytes=64)
+            weave(nc, woven[:], picked)
+            x_w[a, c] = keep.tile([P, CH], U32, name="x_w%d%d" % (a, c), align_bytes=64)
+            x_s[a, c] = keep.tile([P, CH], U8, name="x_s%d%d" % (a, c), align_bytes=64)
+            nc.vector.quantize_mx(out=x_w[a, c][:].bitcast(FP8X4), scales=x_s[a, c][:], in_=woven[:])
+
+        picked0 = keep.tile([P, PACK, J], F32, name="picked0")
+        for i in range(PACK):
+            nc.vector.tensor_tensor(picked0[:, i, :], planes[0, i][:].indirect(offsets[:]), wgt_sb[:], MULT)
+        for c in range(NCH):
+            quantise_x(0, c, picked0[:, :, c * CH : (c + 1) * CH])
+        picked1 = [keep.tile([P, PACK, CH], F32, name="picked1%d" % c) for c in range(NCH)]
+
+        def gather1(i, c):
+            entries = offsets[:, c * CH // LANES : (c + 1) * CH // LANES]
+            nc.vector.tensor_tensor(
+                picked1[c][:, i, :], planes[1, i][:].indirect(entries), wgt_sb[:, c * CH : (c + 1) * CH], MULT
+            )
+
+        for i in range(PACK - 1):
+            for c in range(NCH):
+                gather1(i, c)
+        for c in range(NCH):
+            gather1(PACK - 1, c)
+            quantise_x(1, c, picked1[c][:])
+
+        wd_w = keep.tile([P, 2, PACK, P], I32, name="wd_w", align_bytes=64)
+        wd_s = keep.tile([P, PACK, P], U8, name="wd_s", align_bytes=64)
+        y_w = keep.tile([P, J], I32, name="y_w", align_bytes=64)
+        y_s = keep.tile([P, J], U8, name="y_s", align_bytes=64)
+        out_rows = out_0.rearrange("(p t) j -> p t j", t=PACK)
+        out_words = out_1[0].rearrange("p j i -> p (j i)").bitcast(I32)
+
+        def gate_up(c, jt, h):
+            cols = slice(jt * P, (jt + 1) * P)
+            ga = psum.tile([P, BANK], F32, name="ga", bufs=3)
+            ub = psum.tile([P, BANK], F32, name="ub", bufs=3)
+            for a in range(2):
+                nc.tensor.matmul_mx(
+                    out=ga[:], lhsT=x_w[a, c][:, cols].bitcast(FP8X4), lhsT_scale=x_s[a, c][:, cols],
+                    rhs=wg_w[h][:, a, :].bitcast(FP4X4), rhs_scale=wg_s[:, a, h * BANK : (h + 1) * BANK],
+                    start=a == 0, stop=a == 1,
+                )
+            for a in range(2):
+                nc.tensor.matmul_mx(
+                    out=ub[:], lhsT=x_w[a, c][:, cols].bitcast(FP8X4), lhsT_scale=x_s[a, c][:, cols],
+                    rhs=wu_w[h][:, a, :].bitcast(FP8X4), rhs_scale=wu_s[4 * a :, h * BANK : (h + 1) * BANK],
+                    start=a == 0, stop=a == 1,
+                )
+            act = ring.tile([P, 2, P, 2], F32, name="act")
+            nc.scalar.activation(act[:], ga[:].rearrange("j (p u e) -> j u p e", u=2, e=2), SILU)
+            h_t = ring.tile([P, BANK], BF16, name="h_t", bufs=8, align_bytes=64)
+            nc.vector.tensor_tensor(
+                h_t[:].rearrange("j (u p e) -> j u p e", u=2, e=2),
+                ub[:].rearrange("j (p u e) -> j u p e", u=2, e=2), act[:], MULT,
+            )
+            return h_t
+
+        def turn(c, h_t):
+            woven = ring.tile([P, 2, CH, 2], F32, name="h_woven", bufs=2, align_bytes=64)
+            for a in range(2):
+                turned = psum.tile([P, 2, 2, P], F32, name="turned", tag="aux")
+                for jt in range(2):
+                    words = h_t[c, jt, a][:].bitcast(F32)
+                    for u in range(2):
+                        nc.tensor.transpose(turned[:, jt, u, :], words[:, u * P : (u + 1) * P], ident[:])
+                nc.scalar.copy(
+                    out=woven[:, a].rearrange("p (s j) u -> p s j u", s=2),
+                    in_=turned[:].rearrange("p s u j -> p s j u"),
+                )
+            h_w = ring.tile([P, 2 * CH], U32, name="h_w", bufs=2, align_bytes=64)
+            h_s = ring.tile([P, 2 * CH], U8, name="h_s", bufs=2, align_bytes=64)
+            nc.vector.quantize_mx(
+                out=h_w[:].bitcast(FP8X4), scales=h_s[:],
+                in_=woven[:].rearrange("p a j u -> p (a j u)").bitcast(BF16),
+            )
+            return h_w, h_s
+
+        def down(c, h_w, h_s):
+            y = ring.tile([P, PACK, CH], F32, name="y", bufs=2)
+            for half in range(2):
+                acc = psum.tile([P, 2, CH], F32, name="acc", tag="aux")
+                for s in range(2):
+                    t = 2 * half + s
+                    for a in range(2):
+                        nc.tensor.matmul_mx(
+                            out=acc[:, s, :], lhsT=wd_w[:, a, t, :].bitcast(FP8X4), lhsT_scale=wd_s[4 * a :, t, :],
+                            rhs=h_w[:, a * CH : (a + 1) * CH].bitcast(FP8X4), rhs_scale=h_s[:, a * CH : (a + 1) * CH],
+                            start=a == 0, stop=a == 1,
+                        )
+                nc.vector.tensor_tensor(y[:, 2 * half : 2 * half + 2, :], acc[:], g_c[c][:, 2 * half : 2 * half + 2, :], MULT)
+            cols = slice(c * CH, (c + 1) * CH)
+            nc.sync.dma_start(out_rows[:, :, cols], y[:])
+            y_woven = ring.tile([P, PACK * CH], BF16, name="y_woven", bufs=2, align_bytes=64)
+            weave(nc, y_woven[:], y[:])
+            nc.vector.quantize_mx(out=y_w[:, cols].bitcast(FP8X4), scales=y_s[:, cols], in_=y_woven[:])
+            nc.sync.dma_start(out_words[:, cols], y_w[:, cols])
+
+        h_t, h_q = {}, {}
+        for c in range(NCH + 1):
+            if c < NCH:
+                for h in range(2):
+                    h_t[c, 0, h] = gate_up(c, 0, h)
+            if c == 1:
+                nc.vector.tensor_copy(
+                    out=wd_w[:].rearrange("p a t m -> p a m t"), in_=wd_raw[:].rearrange("p a (m t) -> p a m t", t=PACK)
+                )
+                nc.vector.tensor_copy(
+                    out=wd_s[:].rearrange("p t m -> p m t"), in_=wd_s_raw[:].rearrange("p (m t) -> p m t", t=PACK)
+                )
+            if c > 0:
+                h_q[c - 1] = turn(c - 1, h_t)
+            if c < NCH:
+                for h in range(2):
+                    h_t[c, 1, h] = gate_up(c, 1, h)
+            if c > 0:
+                down(c - 1, *h_q[c - 1])
+        for q in range(4):
+            nc.sync.dma_start(out_2[0, 4 * q : 4 * q + 4, :].bitcast(I32), y_s[32 * q : 32 * q + 4, :].bitcast(I32))

@@ -23,6 +23,7 @@ BANK = 512
 CH = 256
 NCH = J // CH
 LANES = 16
+BUFS = {"ga": 3, "ub": 3, "aux": 2}
 
 
 def weave(nc, dst, src):
@@ -66,19 +67,6 @@ def tile_list_silu_mulP_kernel(
             planes[a, i] = keep.tile([P, T], F32, name="x%d%d" % (a, i))
             nc.sync.dma_start(planes[a, i][:], x_rows[a, i])
 
-        load_plane(0, 0)
-        wgt_sb = keep.tile([P, J], F32, name="wgt_sb")
-        nc.sync.dma_start(wgt_sb[:], wgt)
-        for i in range(1, PACK):
-            load_plane(0, i)
-        for q in range(4):
-            nc.sync.dma_start(
-                wg_s[32 * q : 32 * q + 4].bitcast(I32),
-                wg_scales[:, 4 * q : 4 * q + 4, :].rearrange("a q r -> q a r").bitcast(I32),
-            )
-            nc.sync.dma_start(wu_s[32 * q : 32 * q + 8].bitcast(I32), wu_scales[:, 4 * q : 4 * q + 4, :].bitcast(I32))
-        for i in range(PACK - 1):
-            load_plane(1, i)
         wg_w, wu_w = [], []
 
         def load_w(h):
@@ -93,13 +81,34 @@ def tile_list_silu_mulP_kernel(
                 wu_words.rearrange("a p r i -> p a (r i)")[:, :, 4 * BANK * h : 4 * BANK * (h + 1)].bitcast(I32),
             )
 
+        def load_gate_scales():
+            for q in range(4):
+                nc.sync.dma_start(
+                    wg_s[32 * q : 32 * q + 4].bitcast(I32),
+                    wg_scales[:, 4 * q : 4 * q + 4, :].rearrange("a q r -> q a r").bitcast(I32),
+                )
+
+        def load_packed_scales(plane, scales):
+            for q in range(4):
+                nc.sync.dma_start(plane[32 * q : 32 * q + 8].bitcast(I32), scales[:, 4 * q : 4 * q + 4, :].bitcast(I32))
+
+        load_plane(0, 0)
+        wgt_sb = keep.tile([P, J], F32, name="wgt_sb")
+        nc.sync.dma_start(wgt_sb[:], wgt)
+        load_plane(0, 1)
+        load_plane(0, 2)
+        load_plane(0, 3)
+        load_plane(1, 0)
+        load_plane(1, 1)
+        load_plane(1, 2)
+        load_plane(1, 3)
+        load_gate_scales()
         load_w(0)
-        load_plane(1, PACK - 1)
+        load_packed_scales(wu_s, wu_scales)
         load_w(1)
-        for q in range(4):
-            nc.sync.dma_start(wd_s_raw[32 * q : 32 * q + 8].bitcast(I32), wd_scales[:, 4 * q : 4 * q + 4, :].bitcast(I32))
         wd_raw = keep.tile([P, 2, N], I32, name="wd_raw", align_bytes=64)
         nc.sync.dma_start(wd_raw[:], wd_words.rearrange("a p n i -> p a (n i)").bitcast(I32))
+        load_packed_scales(wd_s_raw, wd_scales)
         g_rows = g.rearrange("(p t) j -> p t j", t=PACK)
         g_c = []
         for c in range(NCH):
@@ -108,32 +117,48 @@ def tile_list_silu_mulP_kernel(
 
         x_w, x_s = {}, {}
 
-        def quantise_x(a, c, picked):
-            woven = keep.tile([P, PACK * CH], BF16, name="xi%d%d" % (a, c), align_bytes=64)
-            weave(nc, woven[:], picked)
-            x_w[a, c] = keep.tile([P, CH], U32, name="x_w%d%d" % (a, c), align_bytes=64)
-            x_s[a, c] = keep.tile([P, CH], U8, name="x_s%d%d" % (a, c), align_bytes=64)
-            nc.vector.quantize_mx(out=x_w[a, c][:].bitcast(FP8X4), scales=x_s[a, c][:], in_=woven[:])
-
-        picked0 = keep.tile([P, PACK, J], F32, name="picked0")
-        for i in range(PACK):
-            nc.vector.tensor_tensor(picked0[:, i, :], planes[0, i][:].indirect(offsets[:]), wgt_sb[:], MULT)
-        for c in range(NCH):
-            quantise_x(0, c, picked0[:, :, c * CH : (c + 1) * CH])
-        picked1 = [keep.tile([P, PACK, CH], F32, name="picked1%d" % c) for c in range(NCH)]
-
-        def gather1(i, c):
-            entries = offsets[:, c * CH // LANES : (c + 1) * CH // LANES]
+        def gather(out, a, i, j0, j1):
             nc.vector.tensor_tensor(
-                picked1[c][:, i, :], planes[1, i][:].indirect(entries), wgt_sb[:, c * CH : (c + 1) * CH], MULT
+                out, planes[a, i][:].indirect(offsets[:, j0 // LANES : j1 // LANES]), wgt_sb[:, j0:j1], MULT
             )
 
+        def quantise_x(a, c, picked, woven):
+            weave(nc, woven, picked)
+            x_w[a, c] = keep.tile([P, CH], U32, name="x_w%d%d" % (a, c), align_bytes=64)
+            x_s[a, c] = keep.tile([P, CH], U8, name="x_s%d%d" % (a, c), align_bytes=64)
+            nc.vector.quantize_mx(out=x_w[a, c][:].bitcast(FP8X4), scales=x_s[a, c][:], in_=woven)
+
+        def fresh_woven(a, c):
+            return keep.tile([P, PACK * CH], BF16, name="xi%d%d" % (a, c), align_bytes=64)[:]
+
+        E0 = 3
+        picked0 = keep.tile([P, PACK, E0 * CH], F32, name="picked0")
         for i in range(PACK - 1):
-            for c in range(NCH):
-                gather1(i, c)
-        for c in range(NCH):
-            gather1(PACK - 1, c)
-            quantise_x(1, c, picked1[c][:])
+            gather(picked0[:, i, :], 0, i, 0, E0 * CH)
+        for c in range(E0):
+            gather(picked0[:, PACK - 1, c * CH : (c + 1) * CH], 0, PACK - 1, c * CH, (c + 1) * CH)
+            quantise_x(0, c, picked0[:, :, c * CH : (c + 1) * CH], fresh_woven(0, c))
+        picked1 = keep.tile([P, PACK, 2 * CH], F32, name="picked1")
+        for i in range(PACK - 1):
+            gather(picked1[:, i, :], 1, i, 0, 2 * CH)
+        late = keep.tile([P, 3 * PACK * BANK], F32, name="late", align_bytes=64)
+        late_jobs = [(1, 2), (0, 3), (1, 3)]
+
+        def row(n):
+            return late[:, n * BANK : (n + 1) * BANK]
+
+        def late_gather(n):
+            a, c = late_jobs[n // PACK]
+            gather(late[:, n * BANK : n * BANK + CH], a, n % PACK, c * CH, (c + 1) * CH)
+            if n % PACK == PACK - 1:
+                rows = late[:, (n - PACK + 1) * BANK : (n + 1) * BANK].rearrange("p (t j) -> p t j", t=PACK)
+                quantise_x(a, c, rows[:, :, :CH], fresh_woven(a, c))
+
+        for c in range(2):
+            gather(picked1[:, PACK - 1, c * CH : (c + 1) * CH], 1, PACK - 1, c * CH, (c + 1) * CH)
+            quantise_x(1, c, picked1[:, :, c * CH : (c + 1) * CH], row(c).bitcast(BF16))
+        for c in range(2):
+            late_gather(c)
 
         wd_w = keep.tile([P, 2, PACK, P], I32, name="wd_w", align_bytes=64)
         wd_s = keep.tile([P, PACK, P], U8, name="wd_s", align_bytes=64)
@@ -141,11 +166,13 @@ def tile_list_silu_mulP_kernel(
         y_s = keep.tile([P, J], U8, name="y_s", align_bytes=64)
         out_rows = out_0.rearrange("(p t) j -> p t j", t=PACK)
         out_words = out_1[0].rearrange("p j i -> p (j i)").bitcast(I32)
+        h_t = {}
 
-        def gate_up(c, jt, h):
-            cols = slice(jt * P, (jt + 1) * P)
-            ga = psum.tile([P, BANK], F32, name="ga", bufs=3)
-            ub = psum.tile([P, BANK], F32, name="ub", bufs=3)
+        def gate_up(jt, h, act=None):
+            c = jt // 2
+            cols = slice(jt % 2 * P, (jt % 2 + 1) * P)
+            ga = psum.tile([P, BANK], F32, name="ga", bufs=BUFS["ga"])
+            ub = psum.tile([P, BANK], F32, name="ub", bufs=BUFS["ub"])
             for a in range(2):
                 nc.tensor.matmul_mx(
                     out=ga[:], lhsT=x_w[a, c][:, cols].bitcast(FP8X4), lhsT_scale=x_s[a, c][:, cols],
@@ -158,73 +185,119 @@ def tile_list_silu_mulP_kernel(
                     rhs=wu_w[h][:, a, :].bitcast(FP8X4), rhs_scale=wu_s[4 * a :, h * BANK : (h + 1) * BANK],
                     start=a == 0, stop=a == 1,
                 )
-            act = ring.tile([P, 2, P, 2], F32, name="act")
-            nc.scalar.activation(act[:], ga[:].rearrange("j (p u e) -> j u p e", u=2, e=2), SILU)
-            h_t = ring.tile([P, BANK], BF16, name="h_t", bufs=8, align_bytes=64)
+            if act is None:
+                act = ring.tile([P, BANK], F32, name="act")[:]
+            order = "j (p u e) -> j u p e"
+            act = act.rearrange("j (u p e) -> j u p e", u=2, e=2)
+            nc.scalar.activation(act, ga[:].rearrange(order, u=2, e=2), SILU)
+            h_t[jt, h] = ring.tile([P, BANK], BF16, name="h_t", bufs=8, align_bytes=64)
             nc.vector.tensor_tensor(
-                h_t[:].rearrange("j (u p e) -> j u p e", u=2, e=2),
-                ub[:].rearrange("j (p u e) -> j u p e", u=2, e=2), act[:], MULT,
+                h_t[jt, h][:].rearrange("j (u p e) -> j u p e", u=2, e=2), ub[:].rearrange(order, u=2, e=2), act, MULT
             )
-            return h_t
 
-        def turn(c, h_t):
-            woven = ring.tile([P, 2, CH, 2], F32, name="h_woven", bufs=2, align_bytes=64)
-            for a in range(2):
-                turned = psum.tile([P, 2, 2, P], F32, name="turned", tag="aux")
-                for jt in range(2):
-                    words = h_t[c, jt, a][:].bitcast(F32)
+        def turn(pairs, tags):
+            n = sum(len(b) for b in pairs)
+            woven = ring.tile([P, n * P, 2], F32, name="h_woven", bufs=3, align_bytes=64)
+            done = 0
+            for bank, tag in zip(pairs, tags):
+                turned = psum.tile([P, len(bank), 2, P], F32, name="turned", tag=tag, bufs=BUFS[tag])
+                for s, pair in enumerate(bank):
+                    words = h_t[pair][:].bitcast(F32)
                     for u in range(2):
-                        nc.tensor.transpose(turned[:, jt, u, :], words[:, u * P : (u + 1) * P], ident[:])
+                        nc.tensor.transpose(turned[:, s, u, :], words[:, u * P : (u + 1) * P], ident[:])
                 nc.scalar.copy(
-                    out=woven[:, a].rearrange("p (s j) u -> p s j u", s=2),
+                    out=woven[:, done * P : (done + len(bank)) * P, :].rearrange("p (s j) u -> p s j u", j=P),
                     in_=turned[:].rearrange("p s u j -> p s j u"),
                 )
-            h_w = ring.tile([P, 2 * CH], U32, name="h_w", bufs=2, align_bytes=64)
-            h_s = ring.tile([P, 2 * CH], U8, name="h_s", bufs=2, align_bytes=64)
+                done += len(bank)
+            h_w = ring.tile([P, n * P], U32, name="h_w", bufs=3, align_bytes=64)
+            h_s = ring.tile([P, n * P], U8, name="h_s", bufs=3, align_bytes=64)
             nc.vector.quantize_mx(
-                out=h_w[:].bitcast(FP8X4), scales=h_s[:],
-                in_=woven[:].rearrange("p a j u -> p (a j u)").bitcast(BF16),
+                out=h_w[:].bitcast(FP8X4), scales=h_s[:], in_=woven[:].rearrange("p j u -> p (j u)").bitcast(BF16)
             )
             return h_w, h_s
 
-        def down(c, h_w, h_s):
-            y = ring.tile([P, PACK, CH], F32, name="y", bufs=2)
-            for half in range(2):
-                acc = psum.tile([P, 2, CH], F32, name="acc", tag="aux")
-                for s in range(2):
-                    t = 2 * half + s
-                    for a in range(2):
-                        nc.tensor.matmul_mx(
-                            out=acc[:, s, :], lhsT=wd_w[:, a, t, :].bitcast(FP8X4), lhsT_scale=wd_s[4 * a :, t, :],
-                            rhs=h_w[:, a * CH : (a + 1) * CH].bitcast(FP8X4), rhs_scale=h_s[:, a * CH : (a + 1) * CH],
-                            start=a == 0, stop=a == 1,
-                        )
-                nc.vector.tensor_tensor(y[:, 2 * half : 2 * half + 2, :], acc[:], g_c[c][:, 2 * half : 2 * half + 2, :], MULT)
-            cols = slice(c * CH, (c + 1) * CH)
+        def down_pass(acc, ts, a, codes, scales):
+            for s, t in enumerate(ts):
+                nc.tensor.matmul_mx(
+                    out=acc[:, s, :], lhsT=wd_w[:, a, t, :].bitcast(FP8X4), lhsT_scale=wd_s[4 * a :, t, :],
+                    rhs=codes.bitcast(FP8X4), rhs_scale=scales,
+                    start=a == 0 and s == 0, stop=a == 1 and s == len(ts) - 1,
+                )
+
+        def finish(j0, width, banks):
+            y = ring.tile([P, PACK, width], F32, name="y", bufs=3)
+            gate = g_c[j0 // CH][:, :, j0 % CH : j0 % CH + width]
+            for acc, ts in banks:
+                nc.vector.tensor_tensor(y[:, ts[0] : ts[-1] + 1, :], acc[:], gate[:, ts[0] : ts[-1] + 1, :], MULT)
+            cols = slice(j0, j0 + width)
             nc.sync.dma_start(out_rows[:, :, cols], y[:])
-            y_woven = ring.tile([P, PACK * CH], BF16, name="y_woven", bufs=2, align_bytes=64)
+            y_woven = ring.tile([P, PACK * width], BF16, name="y_woven", bufs=2, align_bytes=64)
             weave(nc, y_woven[:], y[:])
             nc.vector.quantize_mx(out=y_w[:, cols].bitcast(FP8X4), scales=y_s[:, cols], in_=y_woven[:])
             nc.sync.dma_start(out_words[:, cols], y_w[:, cols])
 
-        h_t, h_q = {}, {}
-        for c in range(NCH + 1):
-            if c < NCH:
-                for h in range(2):
-                    h_t[c, 0, h] = gate_up(c, 0, h)
-            if c == 1:
+        def turn_chunk(c):
+            return turn([[(2 * c, a), (2 * c + 1, a)] for a in range(2)], ["aux", "aux"])
+
+        def down_chunk(c, h_w, h_s):
+            banks = []
+            for half in range(2):
+                acc = psum.tile([P, 2, CH], F32, name="acc", tag="aux", bufs=BUFS["aux"])
+                ts = [2 * half, 2 * half + 1]
+                for a in range(2):
+                    down_pass(acc, ts, a, h_w[:, a * CH : (a + 1) * CH], h_s[:, a * CH : (a + 1) * CH])
+                banks.append((acc, ts))
+            finish(c * CH, CH, banks)
+
+        all_t = list(range(PACK))
+
+        def down_tile(jt, h_w, h_s):
+            acc = psum.tile([P, PACK, P], F32, name="acc", tag="aux", bufs=BUFS["aux"])
+            for a in range(2):
+                down_pass(acc, all_t, a, h_w[:, a * P : (a + 1) * P], h_s[:, a * P : (a + 1) * P])
+            finish(jt * P, P, [(acc, all_t)])
+
+        WIDE = 1
+        units = [(2 * c + s, h) for c in range(WIDE) for h in range(2) for s in range(2)]
+        units += [(jt, h) for jt in range(2 * WIDE, 8) for h in range(2)]
+        h_q = {}
+        for u, (jt, h) in enumerate(units):
+            n = u + 2
+            if n < len(late_jobs) * PACK:
+                gate_up(jt, h, row(n))
+                late_gather(n)
+            else:
+                gate_up(jt, h)
+            if u == 3:
                 nc.vector.tensor_copy(
                     out=wd_w[:].rearrange("p a t m -> p a m t"), in_=wd_raw[:].rearrange("p a (m t) -> p a m t", t=PACK)
                 )
                 nc.vector.tensor_copy(
                     out=wd_s[:].rearrange("p t m -> p m t"), in_=wd_s_raw[:].rearrange("p (m t) -> p m t", t=PACK)
                 )
-            if c > 0:
-                h_q[c - 1] = turn(c - 1, h_t)
-            if c < NCH:
-                for h in range(2):
-                    h_t[c, 1, h] = gate_up(c, 1, h)
-            if c > 0:
-                down(c - 1, *h_q[c - 1])
+            for c in range(WIDE):
+                if u == 4 * c + 3 + 2:
+                    h_q[c] = turn_chunk(c)
+                if u == 4 * c + 3 + 4:
+                    down_chunk(c, *h_q[c])
+            for k in range(2 * WIDE, 7):
+                if u == min(2 * k + 1 + 2, 15):
+                    h_q[k, 0] = turn([[(k, 0), (k, 1)]], ["aux" if k < 6 else "ga"])
+            for k in range(2 * WIDE, 6):
+                if u == min(2 * k + 1 + 4, 15):
+                    down_tile(k, *h_q[k, 0])
+        acc6 = psum.tile([P, PACK, P], F32, name="acc", tag="ub", bufs=BUFS["ub"])
+        h_w, h_s = h_q[6, 0]
+        for a in range(2):
+            down_pass(acc6, all_t, a, h_w[:, a * P : (a + 1) * P], h_s[:, a * P : (a + 1) * P])
+        acc7 = psum.tile([P, PACK, P], F32, name="acc", tag="ga", bufs=BUFS["ga"])
+        h_w, h_s = turn([[(7, 0)]], ["ub"])
+        down_pass(acc7, all_t, 0, h_w[:], h_s[:])
+        finish(6 * P, P, [(acc6, all_t)])
+        h_w, h_s = turn([[(7, 1)]], ["ub"])
+        down_pass(acc7, all_t, 1, h_w[:], h_s[:])
+        finish(7 * P, P, [(acc7, all_t)])
         for q in range(4):
-            nc.sync.dma_start(out_2[0, 4 * q : 4 * q + 4, :].bitcast(I32), y_s[32 * q : 32 * q + 4, :].bitcast(I32))
+            queue = nc.sync if q < 2 else nc.scalar
+            queue.dma_start(out_2[0, 4 * q : 4 * q + 4, :].bitcast(I32), y_s[32 * q : 32 * q + 4, :].bitcast(I32))

@@ -19,15 +19,23 @@ SILU = mybir.ActivationFunctionType.Silu
 
 P = 128
 PACK = 4
+PASSES = 2
 BANK = 512
-CH = 256
-NCH = J // CH
 LANES = 16
-BUFS = {"ga": 3, "ub": 3, "aux": 2}
+QUADRANTS = 4
+TILES = J // P
+LAST = TILES - 1
+
+BANKS = {"ga": 3, "ub": 3, "aux": 2}
+WGT_FIRST = 256
+CUTS = ([0, 512, 1024], [0, 128, 256, 512, 768])
+LATE = CUTS[1][-1]
+GROUPS = [(0, 1), (2, 3), (4,), (5,), (6,)]
+TURN_LAG, DOWN_LAG = 2, 5
 
 
-def weave(nc, dst, src):
-    nc.scalar.copy(
+def weave(copy, dst, src):
+    copy(
         out=dst.rearrange("p (c i t) -> p c t i", i=PACK, t=PACK),
         in_=src.rearrange("p t (c i) -> p c t i", i=PACK),
     )
@@ -40,12 +48,15 @@ def tile_list_silu_mulP_kernel(
     with ExitStack() as ctx:
         keep = ctx.enter_context(tc.tile_pool(name="keep", bufs=1))
         ring = ctx.enter_context(tc.tile_pool(name="ring", bufs=4))
-        psum = ctx.enter_context(tc.psum_pool(name="psum", bufs=2))
+        psum = ctx.enter_context(tc.psum_pool(name="psum", bufs=1))
+
+        def bank(shape, tag):
+            return psum.tile([P] + shape, F32, name=tag, bufs=BANKS[tag])
 
         offsets = keep.tile([P, J // LANES], U16, name="offsets")
         nc.sync.dma_start(offsets[:], offs)
 
-        wg_s = keep.tile([P, 2, R], U8, name="wg_s", align_bytes=64)
+        wg_s = keep.tile([P, PASSES, R], U8, name="wg_s", align_bytes=64)
         wu_s = keep.tile([P, R], U8, name="wu_s", align_bytes=64)
         wd_s_raw = keep.tile([P, N], U8, name="wd_s_raw", align_bytes=64)
         nc.vector.memset(wg_s[:].rearrange("p a r -> p (a r)").bitcast(I32), 0)
@@ -60,244 +71,216 @@ def tile_list_silu_mulP_kernel(
         ident = keep.tile([P, P], F32, name="ident")
         make_identity(nc, ident[:])
 
-        x_rows = xT.rearrange("(a p i) t -> a i p t", a=2, i=PACK)
-        planes = {}
+        x_rows = xT.rearrange("(a p t) c -> a t p c", a=PASSES, t=PACK)
+        planes, wg_w, wu_w = {}, [], []
 
-        def load_plane(a, i):
-            planes[a, i] = keep.tile([P, T], F32, name="x%d%d" % (a, i))
-            nc.sync.dma_start(planes[a, i][:], x_rows[a, i])
+        def load_plane(a, t):
+            planes[a, t] = keep.tile([P, T], F32, name="x%d%d" % (a, t))
+            nc.sync.dma_start(planes[a, t][:], x_rows[a, t])
 
-        wg_w, wu_w = [], []
-
-        def load_w(h):
-            wg_w.append(keep.tile([P, 2, 2 * BANK], U8, name="wg_w%d" % h, align_bytes=64))
+        def load_weights(half):
+            wu_w.append(keep.tile([P, PASSES, BANK], I32, name="wu_w%d" % half, align_bytes=64))
+            wu_bytes = wu_words.rearrange("a p r t -> p a (r t)")
+            nc.sync.dma_start(wu_w[half][:], wu_bytes[:, :, 4 * BANK * half : 4 * BANK * (half + 1)].bitcast(I32))
+            wg_w.append(keep.tile([P, PASSES, 2 * BANK], U8, name="wg_w%d" % half, align_bytes=64))
+            wg_bytes = wg_words.rearrange("a p b -> p a b")
             nc.sync.dma_start(
-                wg_w[h][:].bitcast(I32),
-                wg_words.rearrange("a p b -> p a b")[:, :, 2 * BANK * h : 2 * BANK * (h + 1)].bitcast(I32),
-            )
-            wu_w.append(keep.tile([P, 2, BANK], I32, name="wu_w%d" % h, align_bytes=64))
-            nc.sync.dma_start(
-                wu_w[h][:],
-                wu_words.rearrange("a p r i -> p a (r i)")[:, :, 4 * BANK * h : 4 * BANK * (h + 1)].bitcast(I32),
+                wg_w[half][:].bitcast(I32), wg_bytes[:, :, 2 * BANK * half : 2 * BANK * (half + 1)].bitcast(I32)
             )
 
-        def load_gate_scales():
-            for q in range(4):
-                nc.sync.dma_start(
-                    wg_s[32 * q : 32 * q + 4].bitcast(I32),
-                    wg_scales[:, 4 * q : 4 * q + 4, :].rearrange("a q r -> q a r").bitcast(I32),
-                )
-
-        def load_packed_scales(plane, scales):
-            for q in range(4):
-                nc.sync.dma_start(plane[32 * q : 32 * q + 8].bitcast(I32), scales[:, 4 * q : 4 * q + 4, :].bitcast(I32))
+        def load_shared_scales(dst, scales):
+            for q in range(QUADRANTS):
+                nc.sync.dma_start(dst[32 * q : 32 * q + 8].bitcast(I32), scales[:, 4 * q : 4 * q + 4, :].bitcast(I32))
 
         load_plane(0, 0)
         wgt_sb = keep.tile([P, J], F32, name="wgt_sb")
-        nc.sync.dma_start(wgt_sb[:], wgt)
-        load_plane(0, 1)
-        load_plane(0, 2)
-        load_plane(0, 3)
-        load_plane(1, 0)
-        load_plane(1, 1)
-        load_plane(1, 2)
-        load_plane(1, 3)
-        load_gate_scales()
-        load_w(0)
-        load_packed_scales(wu_s, wu_scales)
-        load_w(1)
-        wd_raw = keep.tile([P, 2, N], I32, name="wd_raw", align_bytes=64)
-        nc.sync.dma_start(wd_raw[:], wd_words.rearrange("a p n i -> p a (n i)").bitcast(I32))
-        load_packed_scales(wd_s_raw, wd_scales)
+        nc.sync.dma_start(wgt_sb[:, :WGT_FIRST], wgt[:, :WGT_FIRST])
+        nc.sync.dma_start(wgt_sb[:, WGT_FIRST:], wgt[:, WGT_FIRST:])
+        for n in range(1, PASSES * PACK):
+            load_plane(n // PACK, n % PACK)
+        load_shared_scales(wu_s, wu_scales)
+        load_weights(0)
+        for q in range(QUADRANTS):
+            nc.sync.dma_start(
+                wg_s[32 * q : 32 * q + 4].bitcast(I32),
+                wg_scales[:, 4 * q : 4 * q + 4, :].rearrange("a q r -> q a r").bitcast(I32),
+            )
+        load_weights(1)
+        wd_raw = keep.tile([P, PASSES, N], I32, name="wd_raw", align_bytes=64)
+        nc.sync.dma_start(wd_raw[:], wd_words.rearrange("a p n t -> p a (n t)").bitcast(I32))
+        load_shared_scales(wd_s_raw, wd_scales)
         g_rows = g.rearrange("(p t) j -> p t j", t=PACK)
-        g_c = []
-        for c in range(NCH):
-            g_c.append(keep.tile([P, PACK, CH], F32, name="g%d" % c))
-            nc.sync.dma_start(g_c[c][:], g_rows[:, :, c * CH : (c + 1) * CH])
+        g_half = []
+        for n in range(2):
+            g_half.append(keep.tile([P, PACK, J // 2], F32, name="g%d" % n, tag="x0%d" % n))
+            nc.sync.dma_start(g_half[n][:], g_rows[:, :, n * J // 2 : (n + 1) * J // 2])
 
         x_w, x_s = {}, {}
 
-        def gather(out, a, i, j0, j1):
-            nc.vector.tensor_tensor(
-                out, planes[a, i][:].indirect(offsets[:, j0 // LANES : j1 // LANES]), wgt_sb[:, j0:j1], MULT
-            )
+        def gather(out, a, t, j0, j1):
+            entries = offsets[:, j0 // LANES : j1 // LANES]
+            nc.vector.tensor_tensor(out, planes[a, t][:].indirect(entries), wgt_sb[:, j0:j1], MULT)
 
-        def quantise_x(a, c, picked, woven):
-            weave(nc, woven, picked)
-            x_w[a, c] = keep.tile([P, CH], U32, name="x_w%d%d" % (a, c), align_bytes=64)
-            x_s[a, c] = keep.tile([P, CH], U8, name="x_s%d%d" % (a, c), align_bytes=64)
-            nc.vector.quantize_mx(out=x_w[a, c][:].bitcast(FP8X4), scales=x_s[a, c][:], in_=woven)
+        def quantise_x(a, j0, j1, picked, woven):
+            weave(nc.scalar.copy, woven, picked)
+            codes = keep.tile([P, j1 - j0], U32, name="x_w%d_%d" % (a, j0), align_bytes=64)
+            scales = keep.tile([P, j1 - j0], U8, name="x_s%d_%d" % (a, j0), align_bytes=64)
+            nc.vector.quantize_mx(out=codes[:].bitcast(FP8X4), scales=scales[:], in_=woven)
+            for tile in range(j0 // P, j1 // P):
+                x_w[a, tile] = codes[:, tile * P - j0 : (tile + 1) * P - j0]
+                x_s[a, tile] = scales[:, tile * P - j0 : (tile + 1) * P - j0]
 
-        def fresh_woven(a, c):
-            return keep.tile([P, PACK * CH], BF16, name="xi%d%d" % (a, c), align_bytes=64)[:]
+        def woven_tile(a, j0, j1):
+            return keep.tile([P, PACK * (j1 - j0)], BF16, name="xg%d_%d" % (a, j0), align_bytes=64)[:]
 
-        E0 = 3
-        picked0 = keep.tile([P, PACK, E0 * CH], F32, name="picked0")
-        for i in range(PACK - 1):
-            gather(picked0[:, i, :], 0, i, 0, E0 * CH)
-        for c in range(E0):
-            gather(picked0[:, PACK - 1, c * CH : (c + 1) * CH], 0, PACK - 1, c * CH, (c + 1) * CH)
-            quantise_x(0, c, picked0[:, :, c * CH : (c + 1) * CH], fresh_woven(0, c))
-        picked1 = keep.tile([P, PACK, 2 * CH], F32, name="picked1")
-        for i in range(PACK - 1):
-            gather(picked1[:, i, :], 1, i, 0, 2 * CH)
-        late = keep.tile([P, 3 * PACK * BANK], F32, name="late", align_bytes=64)
-        late_jobs = [(1, 2), (0, 3), (1, 3)]
+        picked0 = keep.tile([P, PACK, J], F32, name="picked0")
+        gather(picked0[:, 0, :WGT_FIRST], 0, 0, 0, WGT_FIRST)
+        gather(picked0[:, 0, WGT_FIRST:], 0, 0, WGT_FIRST, J)
+        for t in range(1, PACK - 1):
+            gather(picked0[:, t, :], 0, t, 0, J)
+        for j0, j1 in zip(CUTS[0], CUTS[0][1:]):
+            gather(picked0[:, PACK - 1, j0:j1], 0, PACK - 1, j0, j1)
+            quantise_x(0, j0, j1, picked0[:, :, j0:j1], woven_tile(0, j0, j1))
 
-        def row(n):
-            return late[:, n * BANK : (n + 1) * BANK]
+        picked1 = keep.tile([P, PACK, LATE], F32, name="picked1")
+        for t in range(PACK - 1):
+            gather(picked1[:, t, :], 1, t, 0, LATE)
 
-        def late_gather(n):
-            a, c = late_jobs[n // PACK]
-            gather(late[:, n * BANK : n * BANK + CH], a, n % PACK, c * CH, (c + 1) * CH)
-            if n % PACK == PACK - 1:
-                rows = late[:, (n - PACK + 1) * BANK : (n + 1) * BANK].rearrange("p (t j) -> p t j", t=PACK)
-                quantise_x(a, c, rows[:, :, :CH], fresh_woven(a, c))
+        late = keep.tile([P, PACK * BANK], F32, name="late", align_bytes=64)
 
-        for c in range(2):
-            gather(picked1[:, PACK - 1, c * CH : (c + 1) * CH], 1, PACK - 1, c * CH, (c + 1) * CH)
-            quantise_x(1, c, picked1[:, :, c * CH : (c + 1) * CH], row(c).bitcast(BF16))
-        for c in range(2):
-            late_gather(c)
+        def late_row(t):
+            return late[:, t * BANK : (t + 1) * BANK]
 
-        wd_w = keep.tile([P, 2, PACK, P], I32, name="wd_w", align_bytes=64)
+        def late_gather(t):
+            gather(late_row(t)[:, : J - LATE], 1, t, LATE, J)
+
+        for n, (j0, j1) in enumerate(zip(CUTS[1], CUTS[1][1:])):
+            gather(picked1[:, PACK - 1, j0:j1], 1, PACK - 1, j0, j1)
+            woven = late_row(n)[:, : 2 * (j1 - j0)].bitcast(BF16) if n < 2 else woven_tile(1, j0, j1)
+            quantise_x(1, j0, j1, picked1[:, :, j0:j1], woven)
+        late_gather(0)
+        late_gather(1)
+
+        wd_w = keep.tile([P, PASSES, PACK, P], I32, name="wd_w", align_bytes=64)
         wd_s = keep.tile([P, PACK, P], U8, name="wd_s", align_bytes=64)
         y_w = keep.tile([P, J], I32, name="y_w", align_bytes=64)
         y_s = keep.tile([P, J], U8, name="y_s", align_bytes=64)
+        y_woven = keep.tile([P, PACK * J], BF16, name="y_woven", align_bytes=64)
         out_rows = out_0.rearrange("(p t) j -> p t j", t=PACK)
-        out_words = out_1[0].rearrange("p j i -> p (j i)").bitcast(I32)
+        out_words = out_1[0].rearrange("p j t -> p (j t)").bitcast(I32)
         h_t = {}
 
-        def gate_up(jt, h, act=None):
-            c = jt // 2
-            cols = slice(jt % 2 * P, (jt % 2 + 1) * P)
-            ga = psum.tile([P, BANK], F32, name="ga", bufs=BUFS["ga"])
-            ub = psum.tile([P, BANK], F32, name="ub", bufs=BUFS["ub"])
-            for a in range(2):
-                nc.tensor.matmul_mx(
-                    out=ga[:], lhsT=x_w[a, c][:, cols].bitcast(FP8X4), lhsT_scale=x_s[a, c][:, cols],
-                    rhs=wg_w[h][:, a, :].bitcast(FP4X4), rhs_scale=wg_s[:, a, h * BANK : (h + 1) * BANK],
-                    start=a == 0, stop=a == 1,
-                )
-            for a in range(2):
-                nc.tensor.matmul_mx(
-                    out=ub[:], lhsT=x_w[a, c][:, cols].bitcast(FP8X4), lhsT_scale=x_s[a, c][:, cols],
-                    rhs=wu_w[h][:, a, :].bitcast(FP8X4), rhs_scale=wu_s[4 * a :, h * BANK : (h + 1) * BANK],
-                    start=a == 0, stop=a == 1,
-                )
-            if act is None:
-                act = ring.tile([P, BANK], F32, name="act")[:]
-            order = "j (p u e) -> j u p e"
-            act = act.rearrange("j (u p e) -> j u p e", u=2, e=2)
-            nc.scalar.activation(act, ga[:].rearrange(order, u=2, e=2), SILU)
-            h_t[jt, h] = ring.tile([P, BANK], BF16, name="h_t", bufs=8, align_bytes=64)
+        def gate_up(tile, half, act):
+            ga, ub = bank([BANK], "ga"), bank([BANK], "ub")
+            cols = slice(half * BANK, (half + 1) * BANK)
+            gate = (ga, [wg_w[half][:, a, :].bitcast(FP4X4) for a in range(PASSES)],
+                    [wg_s[:, a, cols] for a in range(PASSES)])
+            up = (ub, [wu_w[half][:, a, :].bitcast(FP8X4) for a in range(PASSES)],
+                  [wu_s[4 * a :, cols] for a in range(PASSES)])
+            for acc, words, scales in (gate, up) if tile == LAST else (up, gate):
+                for a in range(PASSES):
+                    nc.tensor.matmul_mx(
+                        out=acc[:], lhsT=x_w[a, tile].bitcast(FP8X4), lhsT_scale=x_s[a, tile],
+                        rhs=words[a], rhs_scale=scales[a], start=a == 0, stop=a == PASSES - 1,
+                    )
+            by_pairs, as_stored = "j (p u e) -> j u p e", "j (u p e) -> j u p e"
+            act = act.rearrange(as_stored, u=2, e=2)
+            nc.scalar.activation(act, ga[:].rearrange(by_pairs, u=2, e=2), SILU)
+            h_t[tile, half] = ring.tile([P, BANK], BF16, name="h_t", bufs=12, align_bytes=64)
             nc.vector.tensor_tensor(
-                h_t[jt, h][:].rearrange("j (u p e) -> j u p e", u=2, e=2), ub[:].rearrange(order, u=2, e=2), act, MULT
+                h_t[tile, half][:].rearrange(as_stored, u=2, e=2), ub[:].rearrange(by_pairs, u=2, e=2), act, MULT
             )
 
-        def turn(pairs, tags):
-            n = sum(len(b) for b in pairs)
-            woven = ring.tile([P, n * P, 2], F32, name="h_woven", bufs=3, align_bytes=64)
-            done = 0
-            for bank, tag in zip(pairs, tags):
-                turned = psum.tile([P, len(bank), 2, P], F32, name="turned", tag=tag, bufs=BUFS[tag])
-                for s, pair in enumerate(bank):
-                    words = h_t[pair][:].bitcast(F32)
+        def turn(parts, tag):
+            woven = ring.tile([P, len(parts) * P, 2], F32, name="h_woven", align_bytes=64)
+            for first in range(0, len(parts), 2):
+                pair = parts[first : first + 2]
+                turned = bank([len(pair), 2, P], tag)
+                for s, part in enumerate(pair):
+                    words = h_t[part][:].bitcast(F32)
                     for u in range(2):
                         nc.tensor.transpose(turned[:, s, u, :], words[:, u * P : (u + 1) * P], ident[:])
                 nc.scalar.copy(
-                    out=woven[:, done * P : (done + len(bank)) * P, :].rearrange("p (s j) u -> p s j u", j=P),
+                    out=woven[:, first * P : (first + len(pair)) * P, :].rearrange("p (s j) u -> p s j u", j=P),
                     in_=turned[:].rearrange("p s u j -> p s j u"),
                 )
-                done += len(bank)
-            h_w = ring.tile([P, n * P], U32, name="h_w", bufs=3, align_bytes=64)
-            h_s = ring.tile([P, n * P], U8, name="h_s", bufs=3, align_bytes=64)
+            h_w = ring.tile([P, len(parts) * P], U32, name="h_w", align_bytes=64)
+            h_s = ring.tile([P, len(parts) * P], U8, name="h_s", align_bytes=64)
             nc.vector.quantize_mx(
                 out=h_w[:].bitcast(FP8X4), scales=h_s[:], in_=woven[:].rearrange("p j u -> p (j u)").bitcast(BF16)
             )
             return h_w, h_s
 
-        def down_pass(acc, ts, a, codes, scales):
-            for s, t in enumerate(ts):
+        def down_pass(acc, slices, a, codes, scales):
+            for s, t in enumerate(slices):
                 nc.tensor.matmul_mx(
                     out=acc[:, s, :], lhsT=wd_w[:, a, t, :].bitcast(FP8X4), lhsT_scale=wd_s[4 * a :, t, :],
                     rhs=codes.bitcast(FP8X4), rhs_scale=scales,
-                    start=a == 0 and s == 0, stop=a == 1 and s == len(ts) - 1,
+                    start=a == 0 and s == 0, stop=a == PASSES - 1 and s == len(slices) - 1,
                 )
 
-        def finish(j0, width, banks):
-            y = ring.tile([P, PACK, width], F32, name="y", bufs=3)
-            gate = g_c[j0 // CH][:, :, j0 % CH : j0 % CH + width]
-            for acc, ts in banks:
-                nc.vector.tensor_tensor(y[:, ts[0] : ts[-1] + 1, :], acc[:], gate[:, ts[0] : ts[-1] + 1, :], MULT)
+        def down(group, quantised, tag):
+            h_w, h_s = quantised
+            width = len(group) * P
+            sums = []
+            for t0 in range(0, PACK, BANK // width):
+                slices = list(range(t0, t0 + BANK // width))
+                acc = bank([len(slices), width], tag)
+                for a in range(PASSES):
+                    down_pass(acc, slices, a, h_w[:, a * width : (a + 1) * width], h_s[:, a * width : (a + 1) * width])
+                sums.append((acc, slices))
+            return sums
+
+        def finish(group, sums):
+            j0, width = group[0] * P, len(group) * P
             cols = slice(j0, j0 + width)
+            y = ring.tile([P, PACK, width], F32, name="y", bufs=len(GROUPS) + 1)
+            gate = g_half[j0 // (J // 2)][:, :, j0 % (J // 2) : j0 % (J // 2) + width]
+            for acc, slices in sums:
+                rows = slice(slices[0], slices[-1] + 1)
+                nc.vector.tensor_tensor(y[:, rows, :], acc[:], gate[:, rows, :], MULT)
             nc.sync.dma_start(out_rows[:, :, cols], y[:])
-            y_woven = ring.tile([P, PACK * width], BF16, name="y_woven", bufs=2, align_bytes=64)
-            weave(nc, y_woven[:], y[:])
-            nc.vector.quantize_mx(out=y_w[:, cols].bitcast(FP8X4), scales=y_s[:, cols], in_=y_woven[:])
+            woven = y_woven[:, PACK * j0 : PACK * (j0 + width)]
+            weave(nc.vector.tensor_copy if group == (LAST,) else nc.scalar.copy, woven, y[:])
+            nc.vector.quantize_mx(out=y_w[:, cols].bitcast(FP8X4), scales=y_s[:, cols], in_=woven)
             nc.sync.dma_start(out_words[:, cols], y_w[:, cols])
 
-        def turn_chunk(c):
-            return turn([[(2 * c, a), (2 * c + 1, a)] for a in range(2)], ["aux", "aux"])
-
-        def down_chunk(c, h_w, h_s):
-            banks = []
-            for half in range(2):
-                acc = psum.tile([P, 2, CH], F32, name="acc", tag="aux", bufs=BUFS["aux"])
-                ts = [2 * half, 2 * half + 1]
-                for a in range(2):
-                    down_pass(acc, ts, a, h_w[:, a * CH : (a + 1) * CH], h_s[:, a * CH : (a + 1) * CH])
-                banks.append((acc, ts))
-            finish(c * CH, CH, banks)
-
-        all_t = list(range(PACK))
-
-        def down_tile(jt, h_w, h_s):
-            acc = psum.tile([P, PACK, P], F32, name="acc", tag="aux", bufs=BUFS["aux"])
-            for a in range(2):
-                down_pass(acc, all_t, a, h_w[:, a * P : (a + 1) * P], h_s[:, a * P : (a + 1) * P])
-            finish(jt * P, P, [(acc, all_t)])
-
-        WIDE = 1
-        units = [(2 * c + s, h) for c in range(WIDE) for h in range(2) for s in range(2)]
-        units += [(jt, h) for jt in range(2 * WIDE, 8) for h in range(2)]
-        h_q = {}
-        for u, (jt, h) in enumerate(units):
-            n = u + 2
-            if n < len(late_jobs) * PACK:
-                gate_up(jt, h, row(n))
-                late_gather(n)
+        steps = [(tile, half) for group in GROUPS + [(LAST,)] for half in range(PASSES) for tile in group]
+        last_step = len(steps) - 1
+        quantised_h = {}
+        for step, (tile, half) in enumerate(steps):
+            if step < 2:
+                gate_up(tile, half, late_row(2 + step))
+                late_gather(2 + step)
             else:
-                gate_up(jt, h)
-            if u == 3:
+                gate_up(tile, half, ring.tile([P, BANK], F32, name="act")[:])
+            if step == 1:
+                late_picked = late[:].rearrange("p (t j) -> p t j", t=PACK)[:, :, : J - LATE]
+                quantise_x(1, LATE, J, late_picked, woven_tile(1, LATE, J))
+            if step == steps.index((GROUPS[0][-1], PASSES - 1)):
                 nc.vector.tensor_copy(
                     out=wd_w[:].rearrange("p a t m -> p a m t"), in_=wd_raw[:].rearrange("p a (m t) -> p a m t", t=PACK)
                 )
                 nc.vector.tensor_copy(
                     out=wd_s[:].rearrange("p t m -> p m t"), in_=wd_s_raw[:].rearrange("p (m t) -> p m t", t=PACK)
                 )
-            for c in range(WIDE):
-                if u == 4 * c + 3 + 2:
-                    h_q[c] = turn_chunk(c)
-                if u == 4 * c + 3 + 4:
-                    down_chunk(c, *h_q[c])
-            for k in range(2 * WIDE, 7):
-                if u == min(2 * k + 1 + 2, 15):
-                    h_q[k, 0] = turn([[(k, 0), (k, 1)]], ["aux" if k < 6 else "ga"])
-            for k in range(2 * WIDE, 6):
-                if u == min(2 * k + 1 + 4, 15):
-                    down_tile(k, *h_q[k, 0])
-        acc6 = psum.tile([P, PACK, P], F32, name="acc", tag="ub", bufs=BUFS["ub"])
-        h_w, h_s = h_q[6, 0]
-        for a in range(2):
-            down_pass(acc6, all_t, a, h_w[:, a * P : (a + 1) * P], h_s[:, a * P : (a + 1) * P])
-        acc7 = psum.tile([P, PACK, P], F32, name="acc", tag="ga", bufs=BUFS["ga"])
-        h_w, h_s = turn([[(7, 0)]], ["ub"])
-        down_pass(acc7, all_t, 0, h_w[:], h_s[:])
-        finish(6 * P, P, [(acc6, all_t)])
-        h_w, h_s = turn([[(7, 1)]], ["ub"])
-        down_pass(acc7, all_t, 1, h_w[:], h_s[:])
-        finish(7 * P, P, [(acc7, all_t)])
-        for q in range(4):
+            for group in GROUPS:
+                if step == steps.index((group[-1], PASSES - 1)) + TURN_LAG:
+                    parts = [(member, a) for a in range(PASSES) for member in group]
+                    quantised_h[group] = turn(parts, "ga" if step == last_step else "aux")
+            for group in GROUPS[:-1]:
+                if step == min(steps.index((group[-1], PASSES - 1)) + DOWN_LAG, last_step):
+                    finish(group, down(group, quantised_h[group], "aux"))
+
+        sums = down(GROUPS[-1], quantised_h[GROUPS[-1]], "ub")
+        every_slice = list(range(PACK))
+        acc = bank([PACK, P], "ga")
+        h_w, h_s = turn([(LAST, 0)], "ub")
+        down_pass(acc, every_slice, 0, h_w[:], h_s[:])
+        finish(GROUPS[-1], sums)
+        h_w, h_s = turn([(LAST, 1)], "ub")
+        down_pass(acc, every_slice, 1, h_w[:], h_s[:])
+        finish((LAST,), [(acc, every_slice)])
+        for q in range(QUADRANTS):
             queue = nc.sync if q < 2 else nc.scalar
             queue.dma_start(out_2[0, 4 * q : 4 * q + 4, :].bitcast(I32), y_s[32 * q : 32 * q + 4, :].bitcast(I32))

from contextlib import ExitStack

import concourse.mybir as mybir
from concourse.masks import make_identity

K, R, N, T, J = 1024, 1024, 512, 2048, 1024
FLOPS = 2 * J * (2 * K * R + R * N)

F32 = mybir.dt.float32
BF16 = mybir.dt.bfloat16
I32 = mybir.dt.int32
U32 = mybir.dt.uint32
U16 = mybir.dt.uint16
U8 = mybir.dt.uint8
FP8X4 = mybir.dt.float8_e4m3fn_x4
FP4X4 = mybir.dt.float4_e2m1fn_x4
MULT = mybir.AluOpType.mult
SILU = mybir.ActivationFunctionType.Silu

P = 128
PACK = 4
PASSES = 2
BANK = 512
LANES = 16
QUADRANTS = 4
TILES = J // P
LAST = TILES - 1

BANKS = {"ga": 3, "ub": 3, "aux": 2}
WGT_FIRST = 256
CUTS = ([0, 512, 1024], [0, 128, 256, 512, 768])
LATE = CUTS[1][-1]
GROUPS = [(0, 1), (2, 3), (4,), (5,), (6,)]
TURN_LAG, DOWN_LAG = 2, 5


def weave(copy, dst, src):
    copy(
        out=dst.rearrange("p (c i t) -> p c t i", i=PACK, t=PACK),
        in_=src.rearrange("p t (c i) -> p c t i", i=PACK),
    )


def tile_list_silu_mulP_kernel(
    tc, xT, wgt, wg_words, wg_scales, wu_words, wu_scales, wd_words, wd_scales, g, offs, out_0, out_1, out_2
):
    nc = tc.nc
    with ExitStack() as ctx:
        keep = ctx.enter_context(tc.tile_pool(name="keep", bufs=1))
        ring = ctx.enter_context(tc.tile_pool(name="ring", bufs=4))
        psum = ctx.enter_context(tc.psum_pool(name="psum", bufs=1))

        def bank(shape, tag):
            return psum.tile([P] + shape, F32, name=tag, bufs=BANKS[tag])

        offsets = keep.tile([P, J // LANES], U16, name="offsets")
        nc.sync.dma_start(offsets[:], offs)

        wg_s = keep.tile([P, PASSES, R], U8, name="wg_s", align_bytes=64)
        wu_s = keep.tile([P, R], U8, name="wu_s", align_bytes=64)
        wd_s_raw = keep.tile([P, N], U8, name="wd_s_raw", align_bytes=64)
        nc.vector.memset(wg_s[:].rearrange("p a r -> p (a r)").bitcast(I32), 0)
        nc.vector.memset(wu_s[:].bitcast(I32), 0)
        nc.vector.memset(wd_s_raw[:].bitcast(I32), 0)

        warm = keep.tile([P, 1], F32, name="warm")
        nc.vector.memset(warm[:], 0.0)
        warm_out = keep.tile([P, 1], F32, name="warm_out")
        nc.scalar.activation(warm_out[:], warm[:], SILU)

        ident = keep.tile([P, P], F32, name="ident")
        make_identity(nc, ident[:])

        x_rows = xT.rearrange("(a p t) c -> a t p c", a=PASSES, t=PACK)
        planes, wg_w, wu_w = {}, [], []

        def load_plane(a, t):
            planes[a, t] = keep.tile([P, T], F32, name="x%d%d" % (a, t))
            nc.sync.dma_start(planes[a, t][:], x_rows[a, t])

        def load_weights(half):
            wu_w.append(keep.tile([P, PASSES, BANK], I32, name="wu_w%d" % half, align_bytes=64))
            wu_bytes = wu_words.rearrange("a p r t -> p a (r t)")
            nc.sync.dma_start(wu_w[half][:], wu_bytes[:, :, 4 * BANK * half : 4 * BANK * (half + 1)].bitcast(I32))
            wg_w.append(keep.tile([P, PASSES, 2 * BANK], U8, name="wg_w%d" % half, align_bytes=64))
            wg_bytes = wg_words.rearrange("a p b -> p a b")
            nc.sync.dma_start(
                wg_w[half][:].bitcast(I32), wg_bytes[:, :, 2 * BANK * half : 2 * BANK * (half + 1)].bitcast(I32)
            )

        def load_shared_scales(dst, scales):
            for q in range(QUADRANTS):
                nc.sync.dma_start(dst[32 * q : 32 * q + 8].bitcast(I32), scales[:, 4 * q : 4 * q + 4, :].bitcast(I32))

        load_plane(0, 0)
        wgt_sb = keep.tile([P, J], F32, name="wgt_sb")
        nc.sync.dma_start(wgt_sb[:, :WGT_FIRST], wgt[:, :WGT_FIRST])
        nc.sync.dma_start(wgt_sb[:, WGT_FIRST:], wgt[:, WGT_FIRST:])
        for n in range(1, PASSES * PACK):
            load_plane(n // PACK, n % PACK)
        load_shared_scales(wu_s, wu_scales)
        load_weights(0)
        for q in range(QUADRANTS):
            nc.sync.dma_start(
                wg_s[32 * q : 32 * q + 4].bitcast(I32),
                wg_scales[:, 4 * q : 4 * q + 4, :].rearrange("a q r -> q a r").bitcast(I32),
            )
        load_weights(1)
        wd_raw = keep.tile([P, PASSES, N], I32, name="wd_raw", align_bytes=64)
        nc.sync.dma_start(wd_raw[:], wd_words.rearrange("a p n t -> p a (n t)").bitcast(I32))
        load_shared_scales(wd_s_raw, wd_scales)
        g_rows = g.rearrange("(p t) j -> p t j", t=PACK)
        g_half = []
        for n in range(2):
            g_half.append(keep.tile([P, PACK, J // 2], F32, name="g%d" % n, tag="x0%d" % n))
            nc.sync.dma_start(g_half[n][:], g_rows[:, :, n * J // 2 : (n + 1) * J // 2])

        x_w, x_s = {}, {}

        def gather(out, a, t, j0, j1):
            entries = offsets[:, j0 // LANES : j1 // LANES]
            nc.vector.tensor_tensor(out, planes[a, t][:].indirect(entries), wgt_sb[:, j0:j1], MULT)

        def quantise_x(a, j0, j1, picked, woven):
            weave(nc.scalar.copy, woven, picked)
            codes = keep.tile([P, j1 - j0], U32, name="x_w%d_%d" % (a, j0), align_bytes=64)
            scales = keep.tile([P, j1 - j0], U8, name="x_s%d_%d" % (a, j0), align_bytes=64)
            nc.vector.quantize_mx(out=codes[:].bitcast(FP8X4), scales=scales[:], in_=woven)
            for tile in range(j0 // P, j1 // P):
                x_w[a, tile] = codes[:, tile * P - j0 : (tile + 1) * P - j0]
                x_s[a, tile] = scales[:, tile * P - j0 : (tile + 1) * P - j0]

        def woven_tile(a, j0, j1):
            return keep.tile([P, PACK * (j1 - j0)], BF16, name="xg%d_%d" % (a, j0), align_bytes=64)[:]

        picked0 = keep.tile([P, PACK, J], F32, name="picked0")
        gather(picked0[:, 0, :WGT_FIRST], 0, 0, 0, WGT_FIRST)
        gather(picked0[:, 0, WGT_FIRST:], 0, 0, WGT_FIRST, J)
        for t in range(1, PACK - 1):
            gather(picked0[:, t, :], 0, t, 0, J)
        for j0, j1 in zip(CUTS[0], CUTS[0][1:]):
            gather(picked0[:, PACK - 1, j0:j1], 0, PACK - 1, j0, j1)
            quantise_x(0, j0, j1, picked0[:, :, j0:j1], woven_tile(0, j0, j1))

        picked1 = keep.tile([P, PACK, LATE], F32, name="picked1")
        for t in range(PACK - 1):
            gather(picked1[:, t, :], 1, t, 0, LATE)

        late = keep.tile([P, PACK * BANK], F32, name="late", align_bytes=64)

        def late_row(t):
            return late[:, t * BANK : (t + 1) * BANK]

        def late_gather(t):
            gather(late_row(t)[:, : J - LATE], 1, t, LATE, J)

        for n, (j0, j1) in enumerate(zip(CUTS[1], CUTS[1][1:])):
            gather(picked1[:, PACK - 1, j0:j1], 1, PACK - 1, j0, j1)
            woven = late_row(n)[:, : 2 * (j1 - j0)].bitcast(BF16) if n < 2 else woven_tile(1, j0, j1)
            quantise_x(1, j0, j1, picked1[:, :, j0:j1], woven)
        late_gather(0)
        late_gather(1)

        wd_w = keep.tile([P, PASSES, PACK, P], I32, name="wd_w", align_bytes=64)
        wd_s = keep.tile([P, PACK, P], U8, name="wd_s", align_bytes=64)
        y_w = keep.tile([P, J], I32, name="y_w", align_bytes=64)
        y_s = keep.tile([P, J], U8, name="y_s", align_bytes=64)
        y_woven = keep.tile([P, PACK * J], BF16, name="y_woven", align_bytes=64)
        out_rows = out_0.rearrange("(p t) j -> p t j", t=PACK)
        out_words = out_1[0].rearrange("p j t -> p (j t)").bitcast(I32)
        h_t = {}

        def gate_up(tile, half, act):
            ga, ub = bank([BANK], "ga"), bank([BANK], "ub")
            cols = slice(half * BANK, (half + 1) * BANK)
            gate = (ga, [wg_w[half][:, a, :].bitcast(FP4X4) for a in range(PASSES)],
                    [wg_s[:, a, cols] for a in range(PASSES)])
            up = (ub, [wu_w[half][:, a, :].bitcast(FP8X4) for a in range(PASSES)],
                  [wu_s[4 * a :, cols] for a in range(PASSES)])
            for acc, words, scales in (gate, up) if tile == LAST else (up, gate):
                for a in range(PASSES):
                    nc.tensor.matmul_mx(
                        out=acc[:], lhsT=x_w[a, tile].bitcast(FP8X4), lhsT_scale=x_s[a, tile],
                        rhs=words[a], rhs_scale=scales[a], start=a == 0, stop=a == PASSES - 1,
                    )
            by_pairs, as_stored = "j (p u e) -> j u p e", "j (u p e) -> j u p e"
            act = act.rearrange(as_stored, u=2, e=2)
            nc.scalar.activation(act, ga[:].rearrange(by_pairs, u=2, e=2), SILU)
            h_t[tile, half] = ring.tile([P, BANK], BF16, name="h_t", bufs=12, align_bytes=64)
            nc.vector.tensor_tensor(
                h_t[tile, half][:].rearrange(as_stored, u=2, e=2), ub[:].rearrange(by_pairs, u=2, e=2), act, MULT
            )

        def turn(parts, tag):
            woven = ring.tile([P, len(parts) * P, 2], F32, name="h_woven", align_bytes=64)
            for first in range(0, len(parts), 2):
                pair = parts[first : first + 2]
                turned = bank([len(pair), 2, P], tag)
                for s, part in enumerate(pair):
                    words = h_t[part][:].bitcast(F32)
                    for u in range(2):
                        nc.tensor.transpose(turned[:, s, u, :], words[:, u * P : (u + 1) * P], ident[:])
                nc.scalar.copy(
                    out=woven[:, first * P : (first + len(pair)) * P, :].rearrange("p (s j) u -> p s j u", j=P),
                    in_=turned[:].rearrange("p s u j -> p s j u"),
                )
            h_w = ring.tile([P, len(parts) * P], U32, name="h_w", align_bytes=64)
            h_s = ring.tile([P, len(parts) * P], U8, name="h_s", align_bytes=64)
            nc.vector.quantize_mx(
                out=h_w[:].bitcast(FP8X4), scales=h_s[:], in_=woven[:].rearrange("p j u -> p (j u)").bitcast(BF16)
            )
            return h_w, h_s

        def down_pass(acc, slices, a, codes, scales):
            for s, t in enumerate(slices):
                nc.tensor.matmul_mx(
                    out=acc[:, s, :], lhsT=wd_w[:, a, t, :].bitcast(FP8X4), lhsT_scale=wd_s[4 * a :, t, :],
                    rhs=codes.bitcast(FP8X4), rhs_scale=scales,
                    start=a == 0 and s == 0, stop=a == PASSES - 1 and s == len(slices) - 1,
                )

        def down(group, quantised, tag):
            h_w, h_s = quantised
            width = len(group) * P
            sums = []
            for t0 in range(0, PACK, BANK // width):
                slices = list(range(t0, t0 + BANK // width))
                acc = bank([len(slices), width], tag)
                for a in range(PASSES):
                    down_pass(acc, slices, a, h_w[:, a * width : (a + 1) * width], h_s[:, a * width : (a + 1) * width])
                sums.append((acc, slices))
            return sums

        def finish(group, sums):
            j0, width = group[0] * P, len(group) * P
            cols = slice(j0, j0 + width)
            y = ring.tile([P, PACK, width], F32, name="y", bufs=len(GROUPS) + 1)
            gate = g_half[j0 // (J // 2)][:, :, j0 % (J // 2) : j0 % (J // 2) + width]
            for acc, slices in sums:
                rows = slice(slices[0], slices[-1] + 1)
                nc.vector.tensor_tensor(y[:, rows, :], acc[:], gate[:, rows, :], MULT)
            nc.sync.dma_start(out_rows[:, :, cols], y[:])
            woven = y_woven[:, PACK * j0 : PACK * (j0 + width)]
            weave(nc.vector.tensor_copy if group == (LAST,) else nc.scalar.copy, woven, y[:])
            nc.vector.quantize_mx(out=y_w[:, cols].bitcast(FP8X4), scales=y_s[:, cols], in_=woven)
            nc.sync.dma_start(out_words[:, cols], y_w[:, cols])

        steps = [(tile, half) for group in GROUPS + [(LAST,)] for half in range(PASSES) for tile in group]
        last_step = len(steps) - 1
        quantised_h = {}
        for step, (tile, half) in enumerate(steps):
            if step < 2:
                gate_up(tile, half, late_row(2 + step))
                late_gather(2 + step)
            else:
                gate_up(tile, half, ring.tile([P, BANK], F32, name="act")[:])
            if step == 1:
                late_picked = late[:].rearrange("p (t j) -> p t j", t=PACK)[:, :, : J - LATE]
                quantise_x(1, LATE, J, late_picked, woven_tile(1, LATE, J))
            if step == steps.index((GROUPS[0][-1], PASSES - 1)):
                nc.vector.tensor_copy(
                    out=wd_w[:].rearrange("p a t m -> p a m t"), in_=wd_raw[:].rearrange("p a (m t) -> p a m t", t=PACK)
                )
                nc.vector.tensor_copy(
                    out=wd_s[:].rearrange("p t m -> p m t"), in_=wd_s_raw[:].rearrange("p (m t) -> p m t", t=PACK)
                )
            for group in GROUPS:
                if step == steps.index((group[-1], PASSES - 1)) + TURN_LAG:
                    parts = [(member, a) for a in range(PASSES) for member in group]
                    quantised_h[group] = turn(parts, "ga" if step == last_step else "aux")
            for group in GROUPS[:-1]:
                if step == min(steps.index((group[-1], PASSES - 1)) + DOWN_LAG, last_step):
                    finish(group, down(group, quantised_h[group], "aux"))

        sums = down(GROUPS[-1], quantised_h[GROUPS[-1]], "ub")
        every_slice = list(range(PACK))
        acc = bank([PACK, P], "ga")
        h_w, h_s = turn([(LAST, 0)], "ub")
        down_pass(acc, every_slice, 0, h_w[:], h_s[:])
        finish(GROUPS[-1], sums)
        h_w, h_s = turn([(LAST, 1)], "ub")
        down_pass(acc, every_slice, 1, h_w[:], h_s[:])
        finish((LAST,), [(acc, every_slice)])
        for q in range(QUADRANTS):
            queue = nc.sync if q < 2 else nc.scalar
            queue.dma_start(out_2[0, 4 * q : 4 * q + 4, :].bitcast(I32), y_s[32 * q : 32 * q + 4, :].bitcast(I32))
